import numpy as np
import ml_dtypes


def mxq(x, axis, fmt="e4m3"):
    dtype, down = {"e4m3": (ml_dtypes.float8_e4m3fn, 7), "e5m2": (ml_dtypes.float8_e5m2, 14)}[fmt]
    v = np.moveaxis(np.asarray(x, np.float32).astype(ml_dtypes.bfloat16).astype(np.float64), axis, -1)
    blocks = v.reshape(v.shape[:-1] + (-1, 32))
    amax = np.abs(blocks).max(-1, keepdims=True)
    byte = np.maximum(np.where(amax > 0, np.frexp(amax)[1] - 1 + 127, 0) - down, 1)
    scale = np.exp2(byte - 127.0)
    codes = (blocks / scale).astype(np.float32).astype(dtype).astype(np.float64)
    return np.moveaxis((codes * scale).reshape(v.shape), -1, axis)


WIDE = False


def mx_kscale(k):
    if not WIDE:
        return np.ones(k)
    levels = np.array([30, -30])
    if k % 512:
        return np.exp2(np.random.permutation(np.resize(levels, k // 32))).repeat(32)
    a = np.empty((k // 512, 16))
    for p in range(k // 512):
        a[p, :8] = np.random.permutation(np.resize(levels, 8))
        for g in range(8):
            far = levels[np.abs(levels - a[p, g]) >= 10]
            a[p, g + 8] = far[np.random.randint(len(far))]
    return np.exp2(a.ravel()).repeat(32)


def f64(x):
    return np.asarray(x).astype(np.float64)


E2M1 = np.array([0.0, 0.5, 1.0, 1.5, 2.0, 3.0, 4.0, 6.0, -0.0, -0.5, -1.0, -1.5, -2.0, -3.0, -4.0, -6.0])


def pack_weight(w, fmt):
    k, n = w.shape
    w = f64(np.asarray(w, np.float32).astype(ml_dtypes.bfloat16)).reshape(k // 32, 32, n)
    amax = np.abs(w).max(1)
    if fmt == "e4m3":
        byte = np.frexp(amax)[1] - 1 + 127 - 7
    else:
        mant, ex = np.frexp(amax / 6.0)
        byte = np.where(mant > 0.5, ex, ex - 1) + 127
    byte = np.clip(np.where(amax > 0, byte, 1), 1, 254)
    scaled = (w * np.exp2(127.0 - byte)[:, None, :]).reshape(k, n).astype(np.float32)
    by_word = np.ascontiguousarray(scaled.reshape(k // 512, 128, 4, n).transpose(0, 1, 3, 2))
    if fmt == "e4m3":
        words = by_word.astype(ml_dtypes.float8_e4m3fn).view(np.uint8)
    else:
        c = by_word.astype(ml_dtypes.float4_e2m1fn).view(np.uint8) & 0xF
        words = (c[..., 0::2] | (c[..., 1::2] << 4)).reshape(k // 512, 128, 2 * n)
    return np.ascontiguousarray(words), np.ascontiguousarray(byte.astype(np.uint8).reshape(k // 512, 16, n))


def unpack_weight(words, scales, fmt):
    g, _, n = scales.shape
    words = np.ascontiguousarray(words).reshape(g, 128, n, -1)
    if fmt == "e4m3":
        vals = words.view(ml_dtypes.float8_e4m3fn).astype(np.float64)
    else:
        nib = np.empty((g, 128, n, 4), np.uint8)
        nib[..., 0::2] = words & 0xF
        nib[..., 1::2] = words >> 4
        vals = E2M1[nib]
    vals = vals * np.repeat(np.exp2(scales.astype(np.float64) - 127.0), 8, axis=1)[..., None]
    return vals.transpose(0, 1, 3, 2).reshape(g * 512, n)


K, L, M, T, N, S = 512, 512, 512, 512, 512, 512


def setup_inputs():
    n = np.random.standard_normal
    fk = mx_kscale(K)
    fl = mx_kscale(L)
    fm = mx_kscale(M)
    fs = mx_kscale(S)
    xtp = pack_weight(n((K, T)) / fk[:, None], "e4m3")
    wap = pack_weight(n((K, M)) * 1 / np.sqrt(K) * fk[:, None], "e2m1")
    xqp = pack_weight(n((L, T)) / fl[:, None], "e4m3")
    wcp = pack_weight(n((L, M)) * 1 / np.sqrt(L) * fl[:, None], "e2m1")
    wtp = pack_weight(n((M, N)) * 1 / np.sqrt(M) / fm[:, None], "e4m3")
    gqp = pack_weight(n((S, T)) / fs[:, None], "e2m1")
    wqp = pack_weight(n((S, N)) * 0.5 / np.sqrt(S) * fs[:, None], "e4m3")
    return {
        "xt_words": xtp[0],
        "xt_scales": xtp[1],
        "wa_words": wap[0],
        "wa_scales": wap[1],
        "xq_words": xqp[0],
        "xq_scales": xqp[1],
        "wc_words": wcp[0],
        "wc_scales": wcp[1],
        "te": (np.random.uniform(-0.9, 0.9, (M, T))).astype(np.float32),
        "us": (np.random.uniform(0.5, 2.0, (M, 1)) * fm[:, None]).astype(np.float32),
        "wt_words": wtp[0],
        "wt_scales": wtp[1],
        "gq_words": gqp[0],
        "gq_scales": gqp[1],
        "wq_words": wqp[0],
        "wq_scales": wqp[1],
    }


def reference(xt_words, xt_scales, wa_words, wa_scales, xq_words, xq_scales, wc_words, wc_scales, te, us, wt_words, wt_scales, gq_words, gq_scales, wq_words, wq_scales):
    xtu = unpack_weight(xt_words, xt_scales, "e4m3")
    wau = unpack_weight(wa_words, wa_scales, "e2m1")
    xqu = unpack_weight(xq_words, xq_scales, "e4m3")
    wcu = unpack_weight(wc_words, wc_scales, "e2m1")
    wtu = unpack_weight(wt_words, wt_scales, "e4m3")
    gqu = unpack_weight(gq_words, gq_scales, "e2m1")
    wqu = unpack_weight(wq_words, wq_scales, "e4m3")
    z = wau.T @ xtu + wcu.T @ xqu
    d = (np.tanh(z) - f64(te)) * f64(us)
    dq = mxq(d, 0, "e5m2")
    y = wtu.T @ dq + wqu.T @ gqu
    return y

@@ -1,0 +1,224 @@
+from contextlib import ExitStack
+
+import concourse.mybir as mybir
+
+K = 512
+FLOPS = 4 * 2 * 512 * 512 * 512
+
+F32 = mybir.dt.float32
+BF16 = mybir.dt.bfloat16
+I32 = mybir.dt.int32
+U32 = mybir.dt.uint32
+U16 = mybir.dt.uint16
+U8 = mybir.dt.uint8
+E4M3 = mybir.dt.float8_e4m3fn_x4
+E5M2 = mybir.dt.float8_e5m2_x4
+E2M1 = mybir.dt.float4_e2m1fn_x4
+ALU = mybir.AluOpType
+ACT = mybir.ActivationFunctionType
+
+P = 128
+PACK = 4
+W = 512
+CH = 128
+NCH = W // CH
+HALF = W // 2
+
+
+def tile_mix_target_error_and_branch_back_kernel(
+    tc, xt_words, xt_scales, wa_words, wa_scales, xq_words, xq_scales, wc_words, wc_scales,
+    te, us, wt_words, wt_scales, gq_words, gq_scales, wq_words, wq_scales, out,
+):
+    nc = tc.nc
+    with ExitStack() as ctx:
+        sb = ctx.enter_context(tc.tile_pool(name="sb", bufs=1))
+        ps = ctx.enter_context(tc.psum_pool(name="ps", bufs=1))
+        ctx.enter_context(tc.manual_schedule())
+
+        def sbt(name, shape, dtype):
+            return sb.tile(shape, dtype, name=name, align_bytes=64)
+
+        xt_w = sbt("xt_w", [P, W], U32)
+        xq_w = sbt("xq_w", [P, W], U32)
+        wt_w = sbt("wt_w", [P, W], U32)
+        wq_w = sbt("wq_w", [P, W], U32)
+        wa_raw = sbt("wa_raw", [P, 2 * W], U8)
+        wc_raw = sbt("wc_raw", [P, 2 * W], U8)
+        wa_w = sbt("wa_w", [P, 2 * W], U8)
+        wc_w = sbt("wc_w", [P, 2 * W], U8)
+        gq_w = sbt("gq_w", [P, 2 * W], U8)
+        early = sbt("early", [P, 4 * W], U8)
+        late = sbt("late", [P, 3 * W], U8)
+        wa_sraw, xt_s, wc_sraw, xq_s = [early[:, i * W:(i + 1) * W] for i in range(4)]
+        wt_s, wq_s, gq_s = [late[:, i * W:(i + 1) * W] for i in range(3)]
+        wa_s = sbt("wa_s", [P, W], U8)
+        wc_s = sbt("wc_s", [P, W], U8)
+        us_t = sbt("us_t", [P, PACK], F32)
+        te_h = [sbt("te%d" % h, [P, PACK, HALF], F32) for h in range(2)]
+        teus = [sbt("teus%d" % h, [P, PACK, HALF], F32) for h in range(2)]
+        th = [sbt("th%d" % c, [P, PACK, CH], F32) for c in range(NCH)]
+        d_rows = [sbt("d_rows%d" % c, [P, PACK, CH], BF16) for c in range(NCH)]
+        d_il = [sbt("d_il%d" % c, [P, CH, PACK], BF16) for c in range(NCH)]
+        dq_w = [sbt("dq_w%d" % c, [P, CH], U32) for c in range(NCH)]
+        dq_s = [sbt("dq_s%d" % c, [P, CH], U8) for c in range(NCH)]
+        res = [sbt("res%d" % c, [P, PACK, CH], F32) for c in range(NCH)]
+        z_ps = [ps.tile([P, PACK, CH], F32, name="z%d" % c) for c in range(NCH)]
+        y_ps = [ps.tile([P, PACK, CH], F32, name="y%d" % c) for c in range(NCH)]
+
+        def load_words8(eng, dst, src):
+            eng.dma_start(out=dst[:].bitcast(I32), in_=src[0].rearrange("p n r -> p (n r)").bitcast(I32))
+
+        def load_words4(eng, dst, src):
+            eng.dma_start(out=dst[:].bitcast(I32), in_=src[0].bitcast(I32))
+
+        def load_scales(eng, plane, src):
+            for q in range(4):
+                eng.dma_start(
+                    out=plane[32 * q:32 * q + 4, :].bitcast(I32),
+                    in_=src[0, 4 * q:4 * q + 4, :].bitcast(I32),
+                )
+
+        def load_te(eng, h):
+            eng.dma_start(
+                out=te_h[h][:],
+                in_=te.rearrange("(p j) t -> p j t", j=PACK)[:, :, h * HALF:(h + 1) * HALF],
+            )
+
+        def perm_words(dst, src):
+            nc.vector.tensor_copy(
+                out=dst[:].bitcast(U16).rearrange("p (j m) -> p j m", j=PACK),
+                in_=src[:].bitcast(U16).rearrange("p (m j) -> p j m", j=PACK),
+            )
+
+        def perm_scales(dst, src):
+            nc.vector.tensor_copy(
+                out=dst[:].rearrange("p (j m) -> p j m", j=PACK),
+                in_=src.rearrange("p (m j) -> p j m", j=PACK),
+            )
+
+        def z_pass(c, w, w_s, x, x_s, first):
+            for j in range(PACK):
+                nc.tensor.matmul_mx(
+                    out=z_ps[c][:, j, :],
+                    lhsT=w[:, 2 * P * j:2 * P * (j + 1)].bitcast(E2M1),
+                    lhsT_scale=w_s[:, P * j:P * (j + 1)],
+                    rhs=x[:, CH * c:CH * (c + 1)].bitcast(E4M3),
+                    rhs_scale=x_s[:, CH * c:CH * (c + 1)],
+                    start=first and j == 0,
+                    stop=(not first) and j == PACK - 1,
+                )
+
+        def branch_pass(c):
+            for a in range(PACK):
+                nc.tensor.matmul_mx(
+                    out=y_ps[c][:, a, :],
+                    lhsT=wq_w[:, P * a:P * (a + 1)].bitcast(E4M3),
+                    lhsT_scale=wq_s[:, P * a:P * (a + 1)],
+                    rhs=gq_w[:, 2 * CH * c:2 * CH * (c + 1)].bitcast(E2M1),
+                    rhs_scale=gq_s[:, CH * c:CH * (c + 1)],
+                    start=a == 0,
+                    stop=False,
+                )
+
+        def error_pass(c):
+            for a in range(PACK):
+                nc.tensor.matmul_mx(
+                    out=y_ps[c][:, a, :],
+                    lhsT=wt_w[:, P * a:P * (a + 1)].bitcast(E4M3),
+                    lhsT_scale=wt_s[:, P * a:P * (a + 1)],
+                    rhs=dq_w[c][:].bitcast(E5M2),
+                    rhs_scale=dq_s[c][:],
+                    start=False,
+                    stop=a == PACK - 1,
+                )
+
+        def weigh_targets(h):
+            for j in range(PACK):
+                nc.vector.tensor_scalar(
+                    out=teus[h][:, j, :], in0=te_h[h][:, j, :], scalar1=us_t[:, j:j + 1], scalar2=None,
+                    op0=ALU.mult,
+                )
+
+        def error_row(c, j):
+            h, o = divmod(c * CH, HALF)
+            nc.vector.scalar_tensor_tensor(
+                out=d_rows[c][:, j, :], in0=th[c][:, j, :], scalar=us_t[:, j:j + 1],
+                in1=teus[h][:, j, o:o + CH], op0=ALU.mult, op1=ALU.subtract,
+            )
+
+        def interleave(c):
+            nc.vector.tensor_copy(
+                out=d_il[c][:].rearrange("p (u i) j -> p u j i", i=4),
+                in_=d_rows[c][:].rearrange("p j (u i) -> p u j i", i=4),
+            )
+
+        def quantise(c):
+            nc.vector.quantize_mx(
+                out=dq_w[c][:].bitcast(E5M2), scales=dq_s[c][:],
+                in_=d_il[c][:].rearrange("p t j -> p (t j)"),
+            )
+
+        def finish(c):
+            nc.scalar.copy(out=res[c][:], in_=y_ps[c][:])
+            nc.sync.dma_start(
+                out=out.rearrange("(a p) t -> p a t", p=P)[:, :, CH * c:CH * (c + 1)], in_=res[c][:],
+            )
+
+        nc.vector.memset(early[:].bitcast(I32), 0)
+        nc.vector.memset(late[:].bitcast(I32), 0)
+
+        load_words4(nc.sync, wa_raw, wa_words)
+        load_words8(nc.scalar, xt_w, xt_words)
+        load_scales(nc.sync, wa_sraw, wa_scales)
+        load_scales(nc.sync, xt_s, xt_scales)
+        load_words4(nc.sync, wc_raw, wc_words)
+        load_scales(nc.sync, wc_sraw, wc_scales)
+        load_words8(nc.sync, xq_w, xq_words)
+        load_scales(nc.sync, xq_s, xq_scales)
+        load_te(nc.sync, 0)
+        load_scales(nc.sync, wq_s, wq_scales)
+        load_words8(nc.sync, wq_w, wq_words)
+        load_words4(nc.sync, gq_w, gq_words)
+        load_te(nc.sync, 1)
+        load_scales(nc.sync, wt_s, wt_scales)
+        load_words8(nc.sync, wt_w, wt_words)
+        nc.gpsimd.dma_start(out=us_t[:], in_=us.rearrange("(p j) o -> p (j o)", j=PACK))
+        load_scales(nc.gpsimd, gq_s, gq_scales)
+
+        perm_words(wa_w, wa_raw)
+        perm_scales(wa_s, wa_sraw)
+        perm_words(wc_w, wc_raw)
+        perm_scales(wc_s, wc_sraw)
+
+        first = lambda c: z_pass(c, wa_w, wa_s, xt_w, xt_s, True)
+        second = lambda c: z_pass(c, wc_w, wc_s, xq_w, xq_s, False)
+        first(0)
+        first(1)
+        first(2)
+        second(0)
+        second(1)
+        first(3)
+        second(2)
+        second(3)
+        for c in range(NCH):
+            nc.scalar.activation(out=th[c][:], in_=z_ps[c][:], func=ACT.Tanh)
+        for c in range(NCH):
+            branch_pass(c)
+
+        weigh_targets(0)
+        for j in range(PACK):
+            error_row(0, j)
+        for c in range(NCH):
+            if c == 1:
+                weigh_targets(1)
+            nxt = [j for j in range(PACK)] if c + 1 < NCH else []
+            for j in nxt[:1]:
+                error_row(c + 1, j)
+            interleave(c)
+            for j in nxt[1:2]:
+                error_row(c + 1, j)
+            quantise(c)
+            for j in nxt[2:]:
+                error_row(c + 1, j)
+            error_pass(c)
+            finish(c)

@@ -2,7 +2,6 @@ from contextlib import ExitStack
 
 import concourse.mybir as mybir
 
-K = 512
 FLOPS = 4 * 2 * 512 * 512 * 512
 
 F32 = mybir.dt.float32
@@ -20,9 +19,10 @@ ACT = mybir.ActivationFunctionType
 P = 128
 PACK = 4
 W = 512
-CH = 128
-NCH = W // CH
 HALF = W // 2
+CHUNKS = ((0, 256), (256, 128), (384, 128))
+Z_BANKS = (((0, 1), (2, 3)), ((0, 1, 2, 3),), ((0, 1, 2, 3),))
+Y_BANKS = (((0, 1), (2, 3)), ((0, 1, 2, 3),), ((0, 1), (2, 3)))
 
 
 def tile_mix_target_error_and_branch_back_kernel(
@@ -35,119 +35,128 @@ def tile_mix_target_error_and_branch_back_kernel(
         ps = ctx.enter_context(tc.psum_pool(name="ps", bufs=1))
         ctx.enter_context(tc.manual_schedule())
 
-        def sbt(name, shape, dtype):
+        def sbuf(name, shape, dtype):
             return sb.tile(shape, dtype, name=name, align_bytes=64)
 
-        xt_w = sbt("xt_w", [P, W], U32)
-        xq_w = sbt("xq_w", [P, W], U32)
-        wt_w = sbt("wt_w", [P, W], U32)
-        wq_w = sbt("wq_w", [P, W], U32)
-        wa_raw = sbt("wa_raw", [P, 2 * W], U8)
-        wc_raw = sbt("wc_raw", [P, 2 * W], U8)
-        wa_w = sbt("wa_w", [P, 2 * W], U8)
-        wc_w = sbt("wc_w", [P, 2 * W], U8)
-        gq_w = sbt("gq_w", [P, 2 * W], U8)
-        early = sbt("early", [P, 4 * W], U8)
-        late = sbt("late", [P, 3 * W], U8)
-        wa_sraw, xt_s, wc_sraw, xq_s = [early[:, i * W:(i + 1) * W] for i in range(4)]
-        wt_s, wq_s, gq_s = [late[:, i * W:(i + 1) * W] for i in range(3)]
-        wa_s = sbt("wa_s", [P, W], U8)
-        wc_s = sbt("wc_s", [P, W], U8)
-        us_t = sbt("us_t", [P, PACK], F32)
-        te_h = [sbt("te%d" % h, [P, PACK, HALF], F32) for h in range(2)]
-        teus = [sbt("teus%d" % h, [P, PACK, HALF], F32) for h in range(2)]
-        th = [sbt("th%d" % c, [P, PACK, CH], F32) for c in range(NCH)]
-        d_rows = [sbt("d_rows%d" % c, [P, PACK, CH], BF16) for c in range(NCH)]
-        d_il = [sbt("d_il%d" % c, [P, CH, PACK], BF16) for c in range(NCH)]
-        dq_w = [sbt("dq_w%d" % c, [P, CH], U32) for c in range(NCH)]
-        dq_s = [sbt("dq_s%d" % c, [P, CH], U8) for c in range(NCH)]
-        res = [sbt("res%d" % c, [P, PACK, CH], F32) for c in range(NCH)]
-        z_ps = [ps.tile([P, PACK, CH], F32, name="z%d" % c) for c in range(NCH)]
-        y_ps = [ps.tile([P, PACK, CH], F32, name="y%d" % c) for c in range(NCH)]
+        xt_w = sbuf("xt_w", [P, W], U32)
+        xq_w = sbuf("xq_w", [P, W], U32)
+        wt_w = sbuf("wt_w", [P, W], U32)
+        wq_w = sbuf("wq_w", [P, W], U32)
+        gq_w = sbuf("gq_w", [P, 2 * W], U8)
+        wa_raw = sbuf("wa_raw", [P, 2 * W], U8)
+        wc_raw = sbuf("wc_raw", [P, 2 * W], U8)
+        wa_w = sbuf("wa_w", [P, 2 * W], U8)
+        wc_w = sbuf("wc_w", [P, 2 * W], U8)
+        planes = sbuf("planes", [P, 7 * W], U8)
+        wa_sraw, xt_s, wc_sraw, xq_s, wt_s, wq_s, gq_s = [planes[:, i * W:(i + 1) * W] for i in range(7)]
+        wa_s = sbuf("wa_s", [P, W], U8)
+        wc_s = sbuf("wc_s", [P, W], U8)
+        us_t = sbuf("us_t", [P, PACK], F32)
+        te_h = [sbuf("te%d" % h, [P, PACK, HALF], F32) for h in range(2)]
+        te_us = [sbuf("te_us%d" % h, [P, PACK, HALF], F32) for h in range(2)]
+        th = [sbuf("th%d" % c, [P, PACK, w], F32) for c, (t0, w) in enumerate(CHUNKS)]
+        d_rows = [sbuf("d_rows%d" % c, [P, PACK, w], BF16) for c, (t0, w) in enumerate(CHUNKS)]
+        d_il = [sbuf("d_il%d" % c, [P, w, PACK], BF16) for c, (t0, w) in enumerate(CHUNKS)]
+        dq_w = [sbuf("dq_w%d" % c, [P, w], U32) for c, (t0, w) in enumerate(CHUNKS)]
+        dq_s = [sbuf("dq_s%d" % c, [P, w], U8) for c, (t0, w) in enumerate(CHUNKS)]
+        z_ps = {}
+        y_ps = {}
+        for c, (t0, w) in enumerate(CHUNKS):
+            for b, rows in enumerate(Z_BANKS[c]):
+                z_ps[c, b] = ps.tile([P, len(rows), w], F32, name="z%d%d" % (c, b))
 
-        def load_words8(eng, dst, src):
-            eng.dma_start(out=dst[:].bitcast(I32), in_=src[0].rearrange("p n r -> p (n r)").bitcast(I32))
+        def load_words8(queue, dst, src):
+            queue.dma_start(out=dst[:].bitcast(I32), in_=src[0].rearrange("p n r -> p (n r)").bitcast(I32))
 
-        def load_words4(eng, dst, src):
-            eng.dma_start(out=dst[:].bitcast(I32), in_=src[0].bitcast(I32))
+        def load_words4(queue, dst, src):
+            queue.dma_start(out=dst[:].bitcast(I32), in_=src[0].bitcast(I32))
 
-        def load_scales(eng, plane, src):
-            for q in range(4):
-                eng.dma_start(
+        def load_scales(queue, plane, src, quadrants):
+            for q in quadrants:
+                queue.dma_start(
                     out=plane[32 * q:32 * q + 4, :].bitcast(I32),
                     in_=src[0, 4 * q:4 * q + 4, :].bitcast(I32),
                 )
 
-        def load_te(eng, h):
-            eng.dma_start(
+        def load_te(h):
+            nc.sync.dma_start(
                 out=te_h[h][:],
                 in_=te.rearrange("(p j) t -> p j t", j=PACK)[:, :, h * HALF:(h + 1) * HALF],
             )
 
-        def perm_words(dst, src):
+        def reorder_columns(words, plane, raw_words, raw_plane):
             nc.vector.tensor_copy(
-                out=dst[:].bitcast(U16).rearrange("p (j m) -> p j m", j=PACK),
-                in_=src[:].bitcast(U16).rearrange("p (m j) -> p j m", j=PACK),
+                out=words[:].bitcast(U16).rearrange("p (j m) -> p j m", j=PACK),
+                in_=raw_words[:].bitcast(U16).rearrange("p (m j) -> p j m", j=PACK),
+            )
+            nc.vector.tensor_copy(
+                out=plane[:].rearrange("p (j m) -> p j m", j=PACK),
+                in_=raw_plane.rearrange("p (m j) -> p j m", j=PACK),
             )
 
-        def perm_scales(dst, src):
-            nc.vector.tensor_copy(
-                out=dst[:].rearrange("p (j m) -> p j m", j=PACK),
-                in_=src.rearrange("p (m j) -> p j m", j=PACK),
-            )
-
-        def z_pass(c, w, w_s, x, x_s, first):
-            for j in range(PACK):
+        def z_product(c, b, w_words, w_plane, x_words, x_plane, opens):
+            t0, w = CHUNKS[c]
+            rows = Z_BANKS[c][b]
+            for i, j in enumerate(rows):
                 nc.tensor.matmul_mx(
-                    out=z_ps[c][:, j, :],
-                    lhsT=w[:, 2 * P * j:2 * P * (j + 1)].bitcast(E2M1),
-                    lhsT_scale=w_s[:, P * j:P * (j + 1)],
-                    rhs=x[:, CH * c:CH * (c + 1)].bitcast(E4M3),
-                    rhs_scale=x_s[:, CH * c:CH * (c + 1)],
-                    start=first and j == 0,
-                    stop=(not first) and j == PACK - 1,
+                    out=z_ps[c, b][:, i, :],
+                    lhsT=w_words[:, 2 * P * j:2 * P * (j + 1)].bitcast(E2M1),
+                    lhsT_scale=w_plane[:, P * j:P * (j + 1)],
+                    rhs=x_words[:, t0:t0 + w].bitcast(E4M3),
+                    rhs_scale=x_plane[:, t0:t0 + w],
+                    start=opens and i == 0,
+                    stop=(not opens) and i == len(rows) - 1,
                 )
 
-        def branch_pass(c):
-            for a in range(PACK):
-                nc.tensor.matmul_mx(
-                    out=y_ps[c][:, a, :],
-                    lhsT=wq_w[:, P * a:P * (a + 1)].bitcast(E4M3),
-                    lhsT_scale=wq_s[:, P * a:P * (a + 1)],
-                    rhs=gq_w[:, 2 * CH * c:2 * CH * (c + 1)].bitcast(E2M1),
-                    rhs_scale=gq_s[:, CH * c:CH * (c + 1)],
-                    start=a == 0,
-                    stop=False,
-                )
+        def z_first(c, b):
+            z_product(c, b, wa_w, wa_s, xt_w, xt_s, True)
 
-        def error_pass(c):
-            for a in range(PACK):
-                nc.tensor.matmul_mx(
-                    out=y_ps[c][:, a, :],
-                    lhsT=wt_w[:, P * a:P * (a + 1)].bitcast(E4M3),
-                    lhsT_scale=wt_s[:, P * a:P * (a + 1)],
-                    rhs=dq_w[c][:].bitcast(E5M2),
-                    rhs_scale=dq_s[c][:],
-                    start=False,
-                    stop=a == PACK - 1,
-                )
+        def z_second(c, b):
+            z_product(c, b, wc_w, wc_s, xq_w, xq_s, False)
 
-        def weigh_targets(h):
-            for j in range(PACK):
-                nc.vector.tensor_scalar(
-                    out=teus[h][:, j, :], in0=te_h[h][:, j, :], scalar1=us_t[:, j:j + 1], scalar2=None,
-                    op0=ALU.mult,
-                )
+        def branch_product(c):
+            t0, w = CHUNKS[c]
+            for b, tiles in enumerate(Y_BANKS[c]):
+                name = "z00" if (c, b) == (2, 1) else "y%d%d" % (c, b)
+                y_ps[c, b] = ps.tile([P, len(tiles), w], F32, name=name)
+                for i, a in enumerate(tiles):
+                    nc.tensor.matmul_mx(
+                        out=y_ps[c, b][:, i, :],
+                        lhsT=wq_w[:, P * a:P * (a + 1)].bitcast(E4M3),
+                        lhsT_scale=wq_s[:, P * a:P * (a + 1)],
+                        rhs=gq_w[:, 2 * t0:2 * (t0 + w)].bitcast(E2M1),
+                        rhs_scale=gq_s[:, t0:t0 + w],
+                        start=i == 0,
+                        stop=False,
+                    )
+
+        def error_product(c):
+            for b, tiles in enumerate(Y_BANKS[c]):
+                for i, a in enumerate(tiles):
+                    nc.tensor.matmul_mx(
+                        out=y_ps[c, b][:, i, :],
+                        lhsT=wt_w[:, P * a:P * (a + 1)].bitcast(E4M3),
+                        lhsT_scale=wt_s[:, P * a:P * (a + 1)],
+                        rhs=dq_w[c][:].bitcast(E5M2),
+                        rhs_scale=dq_s[c][:],
+                        start=False,
+                        stop=i == len(tiles) - 1,
+                    )
+
+        def tanh(c, b):
+            rows = Z_BANKS[c][b]
+            nc.scalar.activation(out=th[c][:, rows[0]:rows[-1] + 1, :], in_=z_ps[c, b][:], func=ACT.Tanh)
 
         def error_row(c, j):
-            h, o = divmod(c * CH, HALF)
+            t0, w = CHUNKS[c]
+            h, o = divmod(t0, HALF)
             nc.vector.scalar_tensor_tensor(
                 out=d_rows[c][:, j, :], in0=th[c][:, j, :], scalar=us_t[:, j:j + 1],
-                in1=teus[h][:, j, o:o + CH], op0=ALU.mult, op1=ALU.subtract,
+                in1=te_us[h][:, j, o:o + w], op0=ALU.mult, op1=ALU.subtract,
             )
 
-        def interleave(c):
-            nc.vector.tensor_copy(
+        def interleave(c, copy):
+            copy(
                 out=d_il[c][:].rearrange("p (u i) j -> p u j i", i=4),
                 in_=d_rows[c][:].rearrange("p j (u i) -> p u j i", i=4),
             )
@@ -158,67 +167,93 @@ def tile_mix_target_error_and_branch_back_kernel(
                 in_=d_il[c][:].rearrange("p t j -> p (t j)"),
             )
 
-        def finish(c):
-            nc.scalar.copy(out=res[c][:], in_=y_ps[c][:])
-            nc.sync.dma_start(
-                out=out.rearrange("(a p) t -> p a t", p=P)[:, :, CH * c:CH * (c + 1)], in_=res[c][:],
+        def store(c, b, copy, queue):
+            t0, w = CHUNKS[c]
+            tiles = Y_BANKS[c][b]
+            res = sbuf("res%d%d" % (c, b), [P, len(tiles), w], F32)
+            copy(out=res[:], in_=y_ps[c, b][:])
+            queue.dma_start(
+                out=out.rearrange("(a p) t -> p a t", p=P)[:, tiles[0]:tiles[-1] + 1, t0:t0 + w],
+                in_=res[:],
             )
 
-        nc.vector.memset(early[:].bitcast(I32), 0)
-        nc.vector.memset(late[:].bitcast(I32), 0)
+        nc.vector.memset(planes[:, 0:2 * W].bitcast(I32), 0)
+        nc.vector.memset(planes[:, 2 * W:4 * W].bitcast(I32), 0)
+        nc.vector.memset(planes[:, 4 * W:7 * W].bitcast(I32), 0)
 
-        load_words4(nc.sync, wa_raw, wa_words)
+        nc.gpsimd.dma_start(out=us_t[:], in_=us.rearrange("(p j) o -> p (j o)", j=PACK))
+        load_scales(nc.gpsimd, wc_sraw, wc_scales, [3, 2])
+        load_scales(nc.gpsimd, gq_s, gq_scales, range(0, 3))
+
+        load_words4(nc.scalar, wa_raw, wa_words)
         load_words8(nc.scalar, xt_w, xt_words)
-        load_scales(nc.sync, wa_sraw, wa_scales)
-        load_scales(nc.sync, xt_s, xt_scales)
+        load_scales(nc.sync, wa_sraw, wa_scales, range(4))
+        load_scales(nc.sync, xt_s, xt_scales, [0])
+        load_te(0)
+        load_scales(nc.sync, xt_s, xt_scales, [1, 2, 3])
         load_words4(nc.sync, wc_raw, wc_words)
-        load_scales(nc.sync, wc_sraw, wc_scales)
+        load_scales(nc.sync, wc_sraw, wc_scales, [0, 1])
         load_words8(nc.sync, xq_w, xq_words)
-        load_scales(nc.sync, xq_s, xq_scales)
-        load_te(nc.sync, 0)
-        load_scales(nc.sync, wq_s, wq_scales)
+        load_scales(nc.sync, xq_s, xq_scales, range(0, 4))
+        load_scales(nc.sync, wq_s, wq_scales, [0, 1])
+        load_te(1)
+        load_scales(nc.sync, wq_s, wq_scales, [2, 3])
+        load_scales(nc.sync, gq_s, gq_scales, range(3, 4))
         load_words8(nc.sync, wq_w, wq_words)
         load_words4(nc.sync, gq_w, gq_words)
-        load_te(nc.sync, 1)
-        load_scales(nc.sync, wt_s, wt_scales)
         load_words8(nc.sync, wt_w, wt_words)
-        nc.gpsimd.dma_start(out=us_t[:], in_=us.rearrange("(p j) o -> p (j o)", j=PACK))
-        load_scales(nc.gpsimd, gq_s, gq_scales)
+        load_scales(nc.sync, wt_s, wt_scales, range(4))
 
-        perm_words(wa_w, wa_raw)
-        perm_scales(wa_s, wa_sraw)
-        perm_words(wc_w, wc_raw)
-        perm_scales(wc_s, wc_sraw)
+        reorder_columns(wa_w, wa_s, wa_raw, wa_sraw)
+        reorder_columns(wc_w, wc_s, wc_raw, wc_sraw)
+        for j in range(PACK):
+            nc.vector.tensor_scalar(
+                out=te_us[0][:, j, :], in0=te_h[0][:, j, :], scalar1=us_t[:, j:j + 1], scalar2=None,
+                op0=ALU.mult,
+            )
 
-        first = lambda c: z_pass(c, wa_w, wa_s, xt_w, xt_s, True)
-        second = lambda c: z_pass(c, wc_w, wc_s, xq_w, xq_s, False)
-        first(0)
-        first(1)
-        first(2)
-        second(0)
-        second(1)
-        first(3)
-        second(2)
-        second(3)
-        for c in range(NCH):
-            nc.scalar.activation(out=th[c][:], in_=z_ps[c][:], func=ACT.Tanh)
-        for c in range(NCH):
-            branch_pass(c)
+        z_first(0, 0)
+        z_first(0, 1)
+        z_first(1, 0)
+        z_second(0, 0)
+        z_second(0, 1)
+        z_second(1, 0)
+        z_first(2, 0)
+        z_second(2, 0)
 
-        weigh_targets(0)
+        tanh(0, 0)
+        tanh(0, 1)
+        tanh(1, 0)
+        for j in range(PACK):
+            nc.scalar.activation(
+                out=te_us[1][:, j, :], in_=te_h[1][:, j, :], func=ACT.Copy, scale=us_t[:, j:j + 1],
+            )
+        tanh(2, 0)
+
         for j in range(PACK):
             error_row(0, j)
-        for c in range(NCH):
-            if c == 1:
-                weigh_targets(1)
-            nxt = [j for j in range(PACK)] if c + 1 < NCH else []
-            for j in nxt[:1]:
-                error_row(c + 1, j)
-            interleave(c)
-            for j in nxt[1:2]:
-                error_row(c + 1, j)
-            quantise(c)
-            for j in nxt[2:]:
-                error_row(c + 1, j)
-            error_pass(c)
-            finish(c)
+        error_row(1, 0)
+        interleave(0, nc.vector.tensor_copy)
+        error_row(1, 1)
+        quantise(0)
+        error_row(1, 2)
+        error_row(1, 3)
+        interleave(1, nc.scalar.copy)
+        for j in range(PACK):
+            error_row(2, j)
+        quantise(1)
+        interleave(2, nc.vector.tensor_copy)
+        quantise(2)
+
+        branch_product(0)
+        error_product(0)
+        branch_product(1)
+        branch_product(2)
+        error_product(1)
+        error_product(2)
+
+        store(0, 0, nc.scalar.copy, nc.sync)
+        store(0, 1, nc.scalar.copy, nc.sync)
+        store(1, 0, nc.vector.tensor_copy, nc.sync)
+        store(2, 0, nc.scalar.copy, nc.scalar)
+        store(2, 1, nc.vector.tensor_copy, nc.sync)

@@ -20,9 +20,15 @@ P = 128
 PACK = 4
 W = 512
 HALF = W // 2
+QUADRANTS = 4
+RUN = 4
+
 CHUNKS = ((0, 256), (256, 128), (384, 128))
+LAST = len(CHUNKS) - 1
 Z_BANKS = (((0, 1), (2, 3)), ((0, 1, 2, 3),), ((0, 1, 2, 3),))
 Y_BANKS = (((0, 1), (2, 3)), ((0, 1, 2, 3),), ((0, 1), (2, 3)))
+WC_ON_GPSIMD = 2
+GQ_ON_GPSIMD = 1
 
 
 def tile_mix_target_error_and_branch_back_kernel(
@@ -65,10 +71,10 @@ def tile_mix_target_error_and_branch_back_kernel(
             for b, rows in enumerate(Z_BANKS[c]):
                 z_ps[c, b] = ps.tile([P, len(rows), w], F32, name="z%d%d" % (c, b))
 
-        def load_words8(queue, dst, src):
+        def load_fp8_words(queue, dst, src):
             queue.dma_start(out=dst[:].bitcast(I32), in_=src[0].rearrange("p n r -> p (n r)").bitcast(I32))
 
-        def load_words4(queue, dst, src):
+        def load_fp4_words(queue, dst, src):
             queue.dma_start(out=dst[:].bitcast(I32), in_=src[0].bitcast(I32))
 
         def load_scales(queue, plane, src, quadrants):
@@ -86,12 +92,12 @@ def tile_mix_target_error_and_branch_back_kernel(
 
         def reorder_columns(words, plane, raw_words, raw_plane):
             nc.vector.tensor_copy(
-                out=words[:].bitcast(U16).rearrange("p (j m) -> p j m", j=PACK),
-                in_=raw_words[:].bitcast(U16).rearrange("p (m j) -> p j m", j=PACK),
+                out=words[:].bitcast(U16).rearrange("p (j i) -> p j i", j=PACK),
+                in_=raw_words[:].bitcast(U16).rearrange("p (i j) -> p j i", j=PACK),
             )
             nc.vector.tensor_copy(
-                out=plane[:].rearrange("p (j m) -> p j m", j=PACK),
-                in_=raw_plane.rearrange("p (m j) -> p j m", j=PACK),
+                out=plane[:].rearrange("p (j i) -> p j i", j=PACK),
+                in_=raw_plane.rearrange("p (i j) -> p j i", j=PACK),
             )
 
         def z_product(c, b, w_words, w_plane, x_words, x_plane, opens):
@@ -117,7 +123,7 @@ def tile_mix_target_error_and_branch_back_kernel(
         def branch_product(c):
             t0, w = CHUNKS[c]
             for b, tiles in enumerate(Y_BANKS[c]):
-                name = "z00" if (c, b) == (2, 1) else "y%d%d" % (c, b)
+                name = "z00" if (c, b) == (LAST, 1) else "y%d%d" % (c, b)
                 y_ps[c, b] = ps.tile([P, len(tiles), w], F32, name=name)
                 for i, a in enumerate(tiles):
                     nc.tensor.matmul_mx(
@@ -157,8 +163,8 @@ def tile_mix_target_error_and_branch_back_kernel(
 
         def interleave(c, copy):
             copy(
-                out=d_il[c][:].rearrange("p (u i) j -> p u j i", i=4),
-                in_=d_rows[c][:].rearrange("p j (u i) -> p u j i", i=4),
+                out=d_il[c][:].rearrange("p (u i) j -> p u j i", i=RUN),
+                in_=d_rows[c][:].rearrange("p j (u i) -> p u j i", i=RUN),
             )
 
         def quantise(c):
@@ -182,27 +188,27 @@ def tile_mix_target_error_and_branch_back_kernel(
         nc.vector.memset(planes[:, 4 * W:7 * W].bitcast(I32), 0)
 
         nc.gpsimd.dma_start(out=us_t[:], in_=us.rearrange("(p j) o -> p (j o)", j=PACK))
-        load_scales(nc.gpsimd, wc_sraw, wc_scales, [3, 2])
-        load_scales(nc.gpsimd, gq_s, gq_scales, range(0, 3))
+        load_scales(nc.gpsimd, wc_sraw, wc_scales, reversed(range(QUADRANTS - WC_ON_GPSIMD, QUADRANTS)))
+        load_scales(nc.gpsimd, gq_s, gq_scales, range(GQ_ON_GPSIMD))
 
-        load_words4(nc.scalar, wa_raw, wa_words)
-        load_words8(nc.scalar, xt_w, xt_words)
-        load_scales(nc.sync, wa_sraw, wa_scales, range(4))
-        load_scales(nc.sync, xt_s, xt_scales, [0])
+        load_fp4_words(nc.scalar, wa_raw, wa_words)
+        load_fp8_words(nc.scalar, xt_w, xt_words)
+        load_scales(nc.sync, wa_sraw, wa_scales, range(QUADRANTS))
+        load_scales(nc.sync, xt_s, xt_scales, range(1))
         load_te(0)
-        load_scales(nc.sync, xt_s, xt_scales, [1, 2, 3])
-        load_words4(nc.sync, wc_raw, wc_words)
-        load_scales(nc.sync, wc_sraw, wc_scales, [0, 1])
-        load_words8(nc.sync, xq_w, xq_words)
-        load_scales(nc.sync, xq_s, xq_scales, range(0, 4))
-        load_scales(nc.sync, wq_s, wq_scales, [0, 1])
+        load_scales(nc.sync, xt_s, xt_scales, range(1, QUADRANTS))
+        load_fp4_words(nc.sync, wc_raw, wc_words)
+        load_scales(nc.sync, wc_sraw, wc_scales, range(QUADRANTS - WC_ON_GPSIMD))
+        load_fp8_words(nc.sync, xq_w, xq_words)
+        load_scales(nc.sync, xq_s, xq_scales, range(QUADRANTS))
+        load_scales(nc.sync, wq_s, wq_scales, range(3))
         load_te(1)
-        load_scales(nc.sync, wq_s, wq_scales, [2, 3])
-        load_scales(nc.sync, gq_s, gq_scales, range(3, 4))
-        load_words8(nc.sync, wq_w, wq_words)
-        load_words4(nc.sync, gq_w, gq_words)
-        load_words8(nc.sync, wt_w, wt_words)
-        load_scales(nc.sync, wt_s, wt_scales, range(4))
+        load_scales(nc.sync, wq_s, wq_scales, range(3, QUADRANTS))
+        load_scales(nc.sync, gq_s, gq_scales, range(GQ_ON_GPSIMD, QUADRANTS))
+        load_fp8_words(nc.sync, wq_w, wq_words)
+        load_fp4_words(nc.sync, gq_w, gq_words)
+        load_fp8_words(nc.sync, wt_w, wt_words)
+        load_scales(nc.sync, wt_s, wt_scales, range(QUADRANTS))
 
         reorder_columns(wa_w, wa_s, wa_raw, wa_sraw)
         reorder_columns(wc_w, wc_s, wc_raw, wc_sraw)
@@ -218,8 +224,8 @@ def tile_mix_target_error_and_branch_back_kernel(
         z_second(0, 0)
         z_second(0, 1)
         z_second(1, 0)
-        z_first(2, 0)
-        z_second(2, 0)
+        z_first(LAST, 0)
+        z_second(LAST, 0)
 
         tanh(0, 0)
         tanh(0, 1)
@@ -228,7 +234,7 @@ def tile_mix_target_error_and_branch_back_kernel(
             nc.scalar.activation(
                 out=te_us[1][:, j, :], in_=te_h[1][:, j, :], func=ACT.Copy, scale=us_t[:, j:j + 1],
             )
-        tanh(2, 0)
+        tanh(LAST, 0)
 
         for j in range(PACK):
             error_row(0, j)
@@ -240,20 +246,20 @@ def tile_mix_target_error_and_branch_back_kernel(
         error_row(1, 3)
         interleave(1, nc.scalar.copy)
         for j in range(PACK):
-            error_row(2, j)
+            error_row(LAST, j)
         quantise(1)
-        interleave(2, nc.vector.tensor_copy)
-        quantise(2)
+        interleave(LAST, nc.vector.tensor_copy)
+        quantise(LAST)
 
         branch_product(0)
         error_product(0)
         branch_product(1)
-        branch_product(2)
+        branch_product(LAST)
         error_product(1)
-        error_product(2)
+        error_product(LAST)
 
         store(0, 0, nc.scalar.copy, nc.sync)
         store(0, 1, nc.scalar.copy, nc.sync)
         store(1, 0, nc.vector.tensor_copy, nc.sync)
-        store(2, 0, nc.scalar.copy, nc.scalar)
-        store(2, 1, nc.vector.tensor_copy, nc.sync)
+        store(LAST, 0, nc.scalar.copy, nc.scalar)
+        store(LAST, 1, nc.vector.tensor_copy, nc.sync)

from contextlib import ExitStack

import concourse.mybir as mybir

FLOPS = 4 * 2 * 512 * 512 * 512

F32 = mybir.dt.float32
BF16 = mybir.dt.bfloat16
I32 = mybir.dt.int32
U32 = mybir.dt.uint32
U16 = mybir.dt.uint16
U8 = mybir.dt.uint8
E4M3 = mybir.dt.float8_e4m3fn_x4
E5M2 = mybir.dt.float8_e5m2_x4
E2M1 = mybir.dt.float4_e2m1fn_x4
ALU = mybir.AluOpType
ACT = mybir.ActivationFunctionType

P = 128
PACK = 4
W = 512
HALF = W // 2
QUADRANTS = 4
RUN = 4

CHUNKS = ((0, 256), (256, 128), (384, 128))
LAST = len(CHUNKS) - 1
Z_BANKS = (((0, 1), (2, 3)), ((0, 1, 2, 3),), ((0, 1, 2, 3),))
Y_BANKS = (((0, 1), (2, 3)), ((0, 1, 2, 3),), ((0, 1), (2, 3)))
WC_ON_GPSIMD = 2
GQ_ON_GPSIMD = 1


def tile_mix_target_error_and_branch_back_kernel(
    tc, xt_words, xt_scales, wa_words, wa_scales, xq_words, xq_scales, wc_words, wc_scales,
    te, us, wt_words, wt_scales, gq_words, gq_scales, wq_words, wq_scales, out,
):
    nc = tc.nc
    with ExitStack() as ctx:
        sb = ctx.enter_context(tc.tile_pool(name="sb", bufs=1))
        ps = ctx.enter_context(tc.psum_pool(name="ps", bufs=1))
        ctx.enter_context(tc.manual_schedule())

        def sbuf(name, shape, dtype):
            return sb.tile(shape, dtype, name=name, align_bytes=64)

        xt_w = sbuf("xt_w", [P, W], U32)
        xq_w = sbuf("xq_w", [P, W], U32)
        wt_w = sbuf("wt_w", [P, W], U32)
        wq_w = sbuf("wq_w", [P, W], U32)
        gq_w = sbuf("gq_w", [P, 2 * W], U8)
        wa_raw = sbuf("wa_raw", [P, 2 * W], U8)
        wc_raw = sbuf("wc_raw", [P, 2 * W], U8)
        wa_w = sbuf("wa_w", [P, 2 * W], U8)
        wc_w = sbuf("wc_w", [P, 2 * W], U8)
        planes = sbuf("planes", [P, 7 * W], U8)
        wa_sraw, xt_s, wc_sraw, xq_s, wt_s, wq_s, gq_s = [planes[:, i * W:(i + 1) * W] for i in range(7)]
        wa_s = sbuf("wa_s", [P, W], U8)
        wc_s = sbuf("wc_s", [P, W], U8)
        us_t = sbuf("us_t", [P, PACK], F32)
        te_h = [sbuf("te%d" % h, [P, PACK, HALF], F32) for h in range(2)]
        te_us = [sbuf("te_us%d" % h, [P, PACK, HALF], F32) for h in range(2)]
        th = [sbuf("th%d" % c, [P, PACK, w], F32) for c, (t0, w) in enumerate(CHUNKS)]
        d_rows = [sbuf("d_rows%d" % c, [P, PACK, w], BF16) for c, (t0, w) in enumerate(CHUNKS)]
        d_il = [sbuf("d_il%d" % c, [P, w, PACK], BF16) for c, (t0, w) in enumerate(CHUNKS)]
        dq_w = [sbuf("dq_w%d" % c, [P, w], U32) for c, (t0, w) in enumerate(CHUNKS)]
        dq_s = [sbuf("dq_s%d" % c, [P, w], U8) for c, (t0, w) in enumerate(CHUNKS)]
        z_ps = {}
        y_ps = {}
        for c, (t0, w) in enumerate(CHUNKS):
            for b, rows in enumerate(Z_BANKS[c]):
                z_ps[c, b] = ps.tile([P, len(rows), w], F32, name="z%d%d" % (c, b))

        def load_fp8_words(queue, dst, src):
            queue.dma_start(out=dst[:].bitcast(I32), in_=src[0].rearrange("p n r -> p (n r)").bitcast(I32))

        def load_fp4_words(queue, dst, src):
            queue.dma_start(out=dst[:].bitcast(I32), in_=src[0].bitcast(I32))

        def load_scales(queue, plane, src, quadrants):
            for q in quadrants:
                queue.dma_start(
                    out=plane[32 * q:32 * q + 4, :].bitcast(I32),
                    in_=src[0, 4 * q:4 * q + 4, :].bitcast(I32),
                )

        def load_te(h):
            nc.sync.dma_start(
                out=te_h[h][:],
                in_=te.rearrange("(p j) t -> p j t", j=PACK)[:, :, h * HALF:(h + 1) * HALF],
            )

        def reorder_columns(words, plane, raw_words, raw_plane):
            nc.vector.tensor_copy(
                out=words[:].bitcast(U16).rearrange("p (j i) -> p j i", j=PACK),
                in_=raw_words[:].bitcast(U16).rearrange("p (i j) -> p j i", j=PACK),
            )
            nc.vector.tensor_copy(
                out=plane[:].rearrange("p (j i) -> p j i", j=PACK),
                in_=raw_plane.rearrange("p (i j) -> p j i", j=PACK),
            )

        def z_product(c, b, w_words, w_plane, x_words, x_plane, opens):
            t0, w = CHUNKS[c]
            rows = Z_BANKS[c][b]
            for i, j in enumerate(rows):
                nc.tensor.matmul_mx(
                    out=z_ps[c, b][:, i, :],
                    lhsT=w_words[:, 2 * P * j:2 * P * (j + 1)].bitcast(E2M1),
                    lhsT_scale=w_plane[:, P * j:P * (j + 1)],
                    rhs=x_words[:, t0:t0 + w].bitcast(E4M3),
                    rhs_scale=x_plane[:, t0:t0 + w],
                    start=opens and i == 0,
                    stop=(not opens) and i == len(rows) - 1,
                )

        def z_first(c, b):
            z_product(c, b, wa_w, wa_s, xt_w, xt_s, True)

        def z_second(c, b):
            z_product(c, b, wc_w, wc_s, xq_w, xq_s, False)

        def branch_product(c):
            t0, w = CHUNKS[c]
            for b, tiles in enumerate(Y_BANKS[c]):
                name = "z00" if (c, b) == (LAST, 1) else "y%d%d" % (c, b)
                y_ps[c, b] = ps.tile([P, len(tiles), w], F32, name=name)
                for i, a in enumerate(tiles):
                    nc.tensor.matmul_mx(
                        out=y_ps[c, b][:, i, :],
                        lhsT=wq_w[:, P * a:P * (a + 1)].bitcast(E4M3),
                        lhsT_scale=wq_s[:, P * a:P * (a + 1)],
                        rhs=gq_w[:, 2 * t0:2 * (t0 + w)].bitcast(E2M1),
                        rhs_scale=gq_s[:, t0:t0 + w],
                        start=i == 0,
                        stop=False,
                    )

        def error_product(c):
            for b, tiles in enumerate(Y_BANKS[c]):
                for i, a in enumerate(tiles):
                    nc.tensor.matmul_mx(
                        out=y_ps[c, b][:, i, :],
                        lhsT=wt_w[:, P * a:P * (a + 1)].bitcast(E4M3),
                        lhsT_scale=wt_s[:, P * a:P * (a + 1)],
                        rhs=dq_w[c][:].bitcast(E5M2),
                        rhs_scale=dq_s[c][:],
                        start=False,
                        stop=i == len(tiles) - 1,
                    )

        def tanh(c, b):
            rows = Z_BANKS[c][b]
            nc.scalar.activation(out=th[c][:, rows[0]:rows[-1] + 1, :], in_=z_ps[c, b][:], func=ACT.Tanh)

        def error_row(c, j):
            t0, w = CHUNKS[c]
            h, o = divmod(t0, HALF)
            nc.vector.scalar_tensor_tensor(
                out=d_rows[c][:, j, :], in0=th[c][:, j, :], scalar=us_t[:, j:j + 1],
                in1=te_us[h][:, j, o:o + w], op0=ALU.mult, op1=ALU.subtract,
            )

        def interleave(c, copy):
            copy(
                out=d_il[c][:].rearrange("p (u i) j -> p u j i", i=RUN),
                in_=d_rows[c][:].rearrange("p j (u i) -> p u j i", i=RUN),
            )

        def quantise(c):
            nc.vector.quantize_mx(
                out=dq_w[c][:].bitcast(E5M2), scales=dq_s[c][:],
                in_=d_il[c][:].rearrange("p t j -> p (t j)"),
            )

        def store(c, b, copy, queue):
            t0, w = CHUNKS[c]
            tiles = Y_BANKS[c][b]
            res = sbuf("res%d%d" % (c, b), [P, len(tiles), w], F32)
            copy(out=res[:], in_=y_ps[c, b][:])
            queue.dma_start(
                out=out.rearrange("(a p) t -> p a t", p=P)[:, tiles[0]:tiles[-1] + 1, t0:t0 + w],
                in_=res[:],
            )

        nc.vector.memset(planes[:, 0:2 * W].bitcast(I32), 0)
        nc.vector.memset(planes[:, 2 * W:4 * W].bitcast(I32), 0)
        nc.vector.memset(planes[:, 4 * W:7 * W].bitcast(I32), 0)

        nc.gpsimd.dma_start(out=us_t[:], in_=us.rearrange("(p j) o -> p (j o)", j=PACK))
        load_scales(nc.gpsimd, wc_sraw, wc_scales, reversed(range(QUADRANTS - WC_ON_GPSIMD, QUADRANTS)))
        load_scales(nc.gpsimd, gq_s, gq_scales, range(GQ_ON_GPSIMD))

        load_fp4_words(nc.scalar, wa_raw, wa_words)
        load_fp8_words(nc.scalar, xt_w, xt_words)
        load_scales(nc.sync, wa_sraw, wa_scales, range(QUADRANTS))
        load_scales(nc.sync, xt_s, xt_scales, range(1))
        load_te(0)
        load_scales(nc.sync, xt_s, xt_scales, range(1, QUADRANTS))
        load_fp4_words(nc.sync, wc_raw, wc_words)
        load_scales(nc.sync, wc_sraw, wc_scales, range(QUADRANTS - WC_ON_GPSIMD))
        load_fp8_words(nc.sync, xq_w, xq_words)
        load_scales(nc.sync, xq_s, xq_scales, range(QUADRANTS))
        load_scales(nc.sync, wq_s, wq_scales, range(3))
        load_te(1)
        load_scales(nc.sync, wq_s, wq_scales, range(3, QUADRANTS))
        load_scales(nc.sync, gq_s, gq_scales, range(GQ_ON_GPSIMD, QUADRANTS))
        load_fp8_words(nc.sync, wq_w, wq_words)
        load_fp4_words(nc.sync, gq_w, gq_words)
        load_fp8_words(nc.sync, wt_w, wt_words)
        load_scales(nc.sync, wt_s, wt_scales, range(QUADRANTS))

        reorder_columns(wa_w, wa_s, wa_raw, wa_sraw)
        reorder_columns(wc_w, wc_s, wc_raw, wc_sraw)
        for j in range(PACK):
            nc.vector.tensor_scalar(
                out=te_us[0][:, j, :], in0=te_h[0][:, j, :], scalar1=us_t[:, j:j + 1], scalar2=None,
                op0=ALU.mult,
            )

        z_first(0, 0)
        z_first(0, 1)
        z_first(1, 0)
        z_second(0, 0)
        z_second(0, 1)
        z_second(1, 0)
        z_first(LAST, 0)
        z_second(LAST, 0)

        tanh(0, 0)
        tanh(0, 1)
        tanh(1, 0)
        for j in range(PACK):
            nc.scalar.activation(
                out=te_us[1][:, j, :], in_=te_h[1][:, j, :], func=ACT.Copy, scale=us_t[:, j:j + 1],
            )
        tanh(LAST, 0)

        for j in range(PACK):
            error_row(0, j)
        error_row(1, 0)
        interleave(0, nc.vector.tensor_copy)
        error_row(1, 1)
        quantise(0)
        error_row(1, 2)
        error_row(1, 3)
        interleave(1, nc.scalar.copy)
        for j in range(PACK):
            error_row(LAST, j)
        quantise(1)
        interleave(LAST, nc.vector.tensor_copy)
        quantise(LAST)

        branch_product(0)
        error_product(0)
        branch_product(1)
        branch_product(LAST)
        error_product(1)
        error_product(LAST)

        store(0, 0, nc.scalar.copy, nc.sync)
        store(0, 1, nc.scalar.copy, nc.sync)
        store(1, 0, nc.vector.tensor_copy, nc.sync)
        store(LAST, 0, nc.scalar.copy, nc.scalar)
        store(LAST, 1, nc.vector.tensor_copy, nc.sync)
